import numpy as np
import ml_dtypes


def mxq(x, axis, fmt="e4m3"):
    dtype, down = {"e4m3": (ml_dtypes.float8_e4m3fn, 7), "e5m2": (ml_dtypes.float8_e5m2, 14)}[fmt]
    v = np.moveaxis(np.asarray(x, np.float32).astype(ml_dtypes.bfloat16).astype(np.float64), axis, -1)
    blocks = v.reshape(v.shape[:-1] + (-1, 32))
    amax = np.abs(blocks).max(-1, keepdims=True)
    byte = np.maximum(np.where(amax > 0, np.frexp(amax)[1] - 1 + 127, 0) - down, 1)
    scale = np.exp2(byte - 127.0)
    codes = (blocks / scale).astype(np.float32).astype(dtype).astype(np.float64)
    return np.moveaxis((codes * scale).reshape(v.shape), -1, axis)


WIDE = False


def mx_kscale(k):
    if not WIDE:
        return np.ones(k)
    levels = np.array([10, -10, 5, -5, 0])
    if k % 512:
        return np.exp2(np.random.permutation(np.resize(levels, k // 32))).repeat(32)
    a = np.empty((k // 512, 16))
    for p in range(k // 512):
        a[p, :8] = np.random.permutation(np.resize(levels, 8))
        for g in range(8):
            far = levels[np.abs(levels - a[p, g]) >= 10]
            a[p, g + 8] = far[np.random.randint(len(far))]
    return np.exp2(a.ravel()).repeat(32)


def f64(x):
    return np.asarray(x).astype(np.float64)


def striped(idx):
    return np.tile(idx.reshape(-1, 16).T, (8, 1)).astype(np.uint16)


def unstriped(offs):
    return offs[:16].T.reshape(-1).astype(np.int64)


def striped8(idx):
    return np.concatenate([x.reshape(-1, 16).T for x in idx]).astype(np.uint16)


def runs(offs, k):
    lists = np.stack([offs[16 * r : 16 * r + 16].T.reshape(-1) for r in range(8)]).astype(np.int64)
    return lists[np.arange(k) % 512 // 64]


def pack_weight(w):
    k, n = w.shape
    w = f64(np.asarray(w, np.float32).astype(ml_dtypes.bfloat16)).reshape(k // 32, 32, n)
    amax = np.abs(w).max(1)
    byte = np.clip(np.where(amax > 0, np.frexp(amax)[1] - 1 + 127 - 7, 1), 1, 254)
    scaled = (w * np.exp2(127.0 - byte)[:, None, :]).reshape(k, n).astype(np.float32)
    words = np.ascontiguousarray(scaled.reshape(k // 512, 128, 4, n).transpose(0, 1, 3, 2)).astype(ml_dtypes.float8_e4m3fn).view(np.uint8)
    return words, np.ascontiguousarray(byte.astype(np.uint8).reshape(k // 512, 16, n))


def unpack_weight(words, scales):
    g, p, n, _ = words.shape
    vals = np.ascontiguousarray(words).view(ml_dtypes.float8_e4m3fn).astype(np.float64) * np.repeat(np.exp2(scales.astype(np.float64) - 127.0), 8, axis=1)[..., None]
    return vals.transpose(0, 1, 3, 2).reshape(g * 512, n)


E2M1 = np.array([0.0, 0.5, 1.0, 1.5, 2.0, 3.0, 4.0, 6.0, -0.0, -0.5, -1.0, -1.5, -2.0, -3.0, -4.0, -6.0])


def pack_fp4(w):
    k, n = w.shape
    w = f64(np.asarray(w, np.float32).astype(ml_dtypes.bfloat16)).reshape(k // 32, 32, n)
    amax = np.abs(w).max(1)
    mant, ex = np.frexp(amax / 6.0)
    byte = np.clip(np.where(amax > 0, np.where(mant > 0.5, ex, ex - 1) + 127, 1), 1, 254)
    scaled = (w * np.exp2(127.0 - byte)[:, None, :]).reshape(k, n).astype(np.float32)
    c = np.ascontiguousarray(scaled.reshape(k // 512, 128, 4, n).transpose(0, 1, 3, 2)).astype(ml_dtypes.float4_e2m1fn).view(np.uint8) & 0xF
    words = (c[..., 0::2] | (c[..., 1::2] << 4)).reshape(k // 512, 128, 2 * n)
    return np.ascontiguousarray(words), np.ascontiguousarray(byte.astype(np.uint8).reshape(k // 512, 16, n))


def unpack_fp4(words, scales):
    g, _, n = scales.shape
    words = np.ascontiguousarray(words).reshape(g, 128, n, 2)
    nib = np.empty((g, 128, n, 4), np.uint8)
    nib[..., 0::2] = words & 0xF
    nib[..., 1::2] = words >> 4
    vals = E2M1[nib] * np.repeat(np.exp2(scales.astype(np.float64) - 127.0), 8, axis=1)[..., None]
    return vals.transpose(0, 1, 3, 2).reshape(g * 512, n)


def sigmoid(v):
    return 1.0 / (1.0 + np.exp(-np.maximum(v, -700.0)))

def planes(y):
    n, m = y.shape
    v = y.astype(np.float32).astype(ml_dtypes.bfloat16).astype(np.float64).reshape(n // 32, 32, m)
    top = np.abs(v).max(1)
    byte = np.clip(np.where(top > 0, np.frexp(top)[1] - 1 + 127 - 7, 1), 1, 254)
    codes = (v * np.exp2(127.0 - byte)[:, None, :]).reshape(n, m).astype(np.float32).astype(ml_dtypes.float8_e4m3fn).view(np.uint8)
    words = codes.reshape(n // 512, 128, 4, m).transpose(0, 1, 3, 2)
    return np.ascontiguousarray(words), np.ascontiguousarray(byte.astype(np.uint8).reshape(n // 512, 16, m))


K, T, S, N, H = 512, 2048, 512, 512, 512


def setup_inputs():
    n = np.random.standard_normal
    s = mx_kscale(K)[:, None]
    u = mx_kscale(H)
    packed_xT = pack_weight(n((K, T)) * s)
    packed_w1 = pack_fp4(n((K, H)) / np.sqrt(K) / s)
    packed_w2 = pack_fp4(n((H, N)) / np.sqrt(H) / u[:, None])
    packed_w3 = pack_fp4(n((H, N)) / np.sqrt(H) / u[:, None])
    return {
        "x_words": packed_xT[0],
        "x_scales": packed_xT[1],
        "w1_words": packed_w1[0],
        "w1_scales": packed_w1[1],
        "gn": (np.random.uniform(0.5, 1.5, (H, 1)) * u[:, None]).astype(np.float32),
        "w2_words": packed_w2[0],
        "w2_scales": packed_w2[1],
        "gm": (np.random.uniform(0.5, 1.5, (H, 1)) * u[:, None]).astype(np.float32),
        "w3_words": packed_w3[0],
        "w3_scales": packed_w3[1],
        "offs": striped(np.random.permutation(T)[:S]),
        "n1": striped8(np.stack([np.random.permutation(S) for _ in range(8)])),
        "n2": striped8(np.stack([np.random.permutation(S) for _ in range(8)])),
        "n3": striped8(np.stack([np.random.permutation(S) for _ in range(8)])),
        "n4": striped8(np.stack([np.random.permutation(S) for _ in range(8)])),
        "n5": striped8(np.stack([np.random.permutation(S) for _ in range(8)])),
        "n6": striped8(np.stack([np.random.permutation(S) for _ in range(8)])),
    }


def reference(x_words, x_scales, w1_words, w1_scales, gn, w2_words, w2_scales, gm, w3_words, w3_scales, offs, n1, n2, n3, n4, n5, n6):
    xq = unpack_weight(x_words, x_scales)[:, unstriped(offs)]
    y = unpack_fp4(w1_words, w1_scales).T @ xq
    z = f64(gn) * ((y[np.arange(H)[:, None], runs(n1, H)]) / (np.abs(y) + np.abs(y[np.arange(H)[:, None], runs(n2, H)]) + 0.5))
    a = unpack_fp4(w2_words, w2_scales).T @ mxq(z, 0, "e4m3")
    z2 = f64(gm) * (np.maximum(y * (sigmoid(y[np.arange(H)[:, None], runs(n3, H)])), y[np.arange(H)[:, None], runs(n4, H)]))
    b = unpack_fp4(w3_words, w3_scales).T @ mxq(z2, 0, "e4m3")
    out_0 = (a - (a[np.arange(N)[:, None], runs(n5, N)])) / (np.abs(b) + np.abs(b[np.arange(N)[:, None], runs(n6, N)]) + 0.5)
    return (out_0,) + planes(out_0)

@@ -1,0 +1,253 @@
+from contextlib import ExitStack
+
+import concourse.mybir as mybir
+
+F32 = mybir.dt.float32
+BF16 = mybir.dt.bfloat16
+I32 = mybir.dt.int32
+U32 = mybir.dt.uint32
+U16 = mybir.dt.uint16
+U8 = mybir.dt.uint8
+FP8X4 = mybir.dt.float8_e4m3fn_x4
+FP4X4 = mybir.dt.float4_e2m1fn_x4
+ACT = mybir.ActivationFunctionType
+ALU = mybir.AluOpType
+
+P = 128
+PACK = 4
+T = 2048
+S = 512
+HALF = S // 2
+FLOPS = 3 * 2 * 512 * 512 * 512
+
+
+def tile_picked_forknormbnorm2gmax_none_po_kernel(
+    tc, x_words, x_scales, w1_words, w1_scales, gn, w2_words, w2_scales, gm, w3_words, w3_scales,
+    offs, n1, n2, n3, n4, n5, n6, out_0, out_1, out_2,
+):
+    nc = tc.nc
+    with ExitStack() as ctx:
+        keep = ctx.enter_context(tc.tile_pool(name="keep", bufs=1))
+        psum = ctx.enter_context(tc.psum_pool(name="psum", bufs=1))
+
+        def load_list(name, src):
+            tile = keep.tile([P, S // 16], U16, name=name)
+            nc.sync.dma_start(tile[:], src)
+            return tile
+
+        def zeroed_plane(name, width, engine):
+            tile = keep.tile([P, width], U8, name=name, tag=name, align_bytes=64)
+            engine.memset(tile[:].bitcast(I32), 0)
+            return tile
+
+        def load_plane(tile, src, quadrants=range(4), engine=nc.sync):
+            rows = src[0].bitcast(I32)
+            for q in quadrants:
+                engine.dma_start(tile[32 * q : 32 * q + 4, :].bitcast(I32), rows[4 * q : 4 * q + 4, :])
+
+        def load_words(name, src):
+            tile = keep.tile([P, 2 * S], U8, name=name, align_bytes=64)
+            nc.sync.dma_start(tile[:].bitcast(I32), src[0].bitcast(I32))
+            return tile
+
+        def load_gain(name, src):
+            tile = keep.tile([P, PACK], F32, name=name)
+            nc.sync.dma_start(tile[:], src.rearrange("(p t) o -> p (t o)", t=PACK))
+            return tile
+
+        def deal(name, words, plane):
+            dealt_words = keep.tile([P, 2 * S], U8, name=name + "_words", align_bytes=64)
+            dealt_plane = keep.tile([P, S], U8, name=name + "_plane", align_bytes=64)
+            nc.vector.tensor_copy(
+                dealt_words[:].rearrange("p (t m b) -> p t m b", t=PACK, b=2),
+                words[:].rearrange("p (m t b) -> p t m b", t=PACK, b=2),
+            )
+            nc.vector.tensor_copy(
+                dealt_plane[:].rearrange("p (t m) -> p t m", t=PACK),
+                plane[:].rearrange("p (m t) -> p t m", t=PACK),
+            )
+            return dealt_words, dealt_plane
+
+        def product(first_bank, weights, codes, plane):
+            words, scales = weights
+            banks = []
+            for t in range(PACK):
+                bank = psum.tile([P, S], F32, name="bank", tag="bank%d" % (first_bank + t))
+                nc.tensor.matmul_mx(
+                    out=bank[:],
+                    lhsT=words[:, 2 * P * t : 2 * P * (t + 1)].bitcast(FP4X4),
+                    lhsT_scale=scales[:, P * t : P * (t + 1)],
+                    rhs=codes[:].bitcast(FP8X4),
+                    rhs_scale=plane[:],
+                    start=True,
+                    stop=True,
+                )
+                banks.append(bank)
+            return banks
+
+        def rows4(name, width=S):
+            return keep.tile([P, PACK, width], F32, name=name)
+
+        def windows(name):
+            return [keep.tile([P, 2 * S], F32, name="%s%d" % (name, t)) for t in range(PACK)]
+
+        def woven_in(tile):
+            return tile[:].rearrange("p t (c i) -> p c t i", i=4)
+
+        def woven_out(tile):
+            return tile[:].rearrange("p (c i t) -> p c t i", i=4, t=PACK)
+
+        def gain_and_quantize(name, values, gain):
+            rounded = keep.tile([P, PACK * S], BF16, name=name + "_bf16", align_bytes=64)
+            codes = keep.tile([P, S], U32, name=name + "_codes", align_bytes=64)
+            plane = keep.tile([P, S], U8, name=name + "_plane", align_bytes=64)
+            spread = gain[:].unsqueeze(1).unsqueeze(3).to_broadcast([P, S // 4, PACK, 4])
+            nc.vector.tensor_tensor(woven_out(rounded), woven_in(values), spread, ALU.mult)
+            nc.vector.quantize_mx(out=codes[:].bitcast(FP8X4), scales=plane[:], in_=rounded[:])
+            return codes, plane
+
+        def magnitudes(wins, banks):
+            for t in range(PACK):
+                nc.scalar.activation(wins[t][:, :S], banks[t][:], ACT.Abs)
+                nc.sync.dma_start(wins[t ^ 1][:, S:], wins[t][:, :S])
+
+        def reciprocal(recip, root, total):
+            nc.scalar.activation(root, total, ACT.Abs_reciprocal_sqrt, bias=0.5)
+            nc.scalar.activation(recip, root, ACT.Square)
+
+        halves = [slice(HALF * h, HALF * (h + 1)) for h in range(2)]
+        half_lists = [slice(16 * h, 16 * (h + 1)) for h in range(2)]
+
+        w1s_raw = zeroed_plane("w1s_raw", S, nc.gpsimd)
+        xs_raw = zeroed_plane("xs_raw", T, nc.vector)
+        offs_t = load_list("offs", offs)
+        w1w_raw = load_words("w1w_raw", w1_words)
+        load_plane(w1s_raw, w1_scales, range(1))
+        xw_raw = keep.tile([P, T], U32, name="xw_raw")
+        nc.sync.dma_start(xw_raw[:].bitcast(I32), x_words[0].rearrange("p n t -> p (n t)").bitcast(I32))
+        load_plane(xs_raw, x_scales, range(4), nc.scalar)
+        load_plane(w1s_raw, w1_scales, range(1, 4))
+        warm = keep.tile([P, 3], F32, name="warm")
+        nc.gpsimd.memset(warm[:, 0:1], 0.0)
+        nc.scalar.activation(warm[:, 1:2], warm[:, 0:1], ACT.Sigmoid)
+        w3s_raw = zeroed_plane("w3s_raw", S, nc.gpsimd)
+        w2s_raw = zeroed_plane("w2s_raw", S, nc.gpsimd)
+        n4_t = load_list("n4", n4)
+        w3w_raw = load_words("w3w_raw", w3_words)
+        n3_t = load_list("n3", n3)
+        load_plane(w3s_raw, w3_scales)
+        gm_t = load_gain("gm", gm)
+        w2w_raw = load_words("w2w_raw", w2_words)
+        load_plane(w2s_raw, w2_scales)
+        gn_t = load_gain("gn", gn)
+        n2_t = load_list("n2", n2)
+        n1_t = load_list("n1", n1)
+        n6_t = load_list("n6", n6)
+        n5_t = load_list("n5", n5)
+
+        vals = windows("vals")
+        for t in range(PACK):
+            nc.vector.memset(vals[t][:, S:], 0.0)
+
+        w1 = deal("w1", w1w_raw, w1s_raw)
+        x_plane = keep.tile([P, S], U8, name="x_plane", align_bytes=64)
+        nc.vector.tensor_copy(x_plane[:], xs_raw[:].indirect(offs_t[:]))
+        x_codes = keep.tile([P, S], U32, name="x_codes", tag="xs_raw", align_bytes=64)
+        nc.vector.tensor_copy(x_codes[:], xw_raw[:].indirect(offs_t[:]))
+        y_banks = product(0, w1, x_codes, x_plane)
+        w3 = deal("w3", w3w_raw, w3s_raw)
+        for t in range(PACK):
+            nc.scalar.copy(vals[t][:, :S], y_banks[t][:])
+
+        other = rows4("other")
+        gate = rows4("gate")
+        gated = rows4("gated")
+        larger = rows4("larger")
+        for t in range(PACK):
+            nc.vector.tensor_copy(other[:, t, :], vals[t][:].indirect(n4_t[:]))
+        for t in range(PACK):
+            nc.scalar.activation(gate[:, t, :], vals[t][:].indirect(n3_t[:]), ACT.Sigmoid)
+        y_size = windows("y_size")
+        magnitudes(y_size, y_banks)
+        gained = [keep.tile([P, S], F32, name="gained%d" % t) for t in range(PACK)]
+        for t in range(PACK):
+            nc.scalar.activation(gained[t][:], y_banks[t][:], ACT.Copy, scale=gn_t[:, t : t + 1])
+        nc.scalar.activation(warm[:, 2:3], gate[:, PACK - 1, 0:1], ACT.Abs_reciprocal_sqrt, bias=0.5)
+        for t in range(PACK):
+            nc.vector.tensor_tensor(gated[:, t, :], gate[:, t, :], vals[t][:, :S], ALU.mult)
+        nc.vector.tensor_tensor(larger[:], gated[:], other[:], ALU.max)
+        z2_codes, z2_plane = gain_and_quantize("z2", larger, gm_t)
+        b_banks = product(4, w3, z2_codes, z2_plane)
+        w2 = deal("w2", w2w_raw, w2s_raw)
+
+        y_sum = rows4("y_sum")
+        root = rows4("root")
+        y_recip = rows4("y_recip")
+        b_size = windows("b_size")
+        for t in range(PACK):
+            nc.vector.tensor_tensor(y_sum[:, t, :], y_size[t][:].indirect(n2_t[:]), y_size[t ^ 1][:, S:], ALU.add)
+        for t in range(PACK):
+            reciprocal(y_recip[:, t, halves[0]], root[:, t, halves[0]], y_sum[:, t, halves[0]])
+            if t < 2:
+                for u in (2 * t, 2 * t + 1):
+                    nc.scalar.activation(b_size[u][:, :S], b_banks[u][:], ACT.Abs)
+                    nc.sync.dma_start(b_size[u ^ 1][:, S:], b_size[u][:, :S])
+        for t in range(PACK):
+            reciprocal(y_recip[:, t, halves[1]], root[:, t, halves[1]], y_sum[:, t, halves[1]])
+        z_bf16 = keep.tile([P, PACK * S], BF16, name="z_bf16", tag="z_bf16", align_bytes=64)
+        for h in range(2):
+            ratio = keep.tile([P, PACK, HALF], F32, name="ratio", tag="ratio%d" % h)
+            for t in range(PACK):
+                nc.vector.tensor_tensor(
+                    ratio[:, t, :], gained[t][:].indirect(n1_t[:, half_lists[h]]), y_recip[:, t, halves[h]], ALU.mult
+                )
+            nc.scalar.copy(woven_out(z_bf16[:, PACK * HALF * h : PACK * HALF * (h + 1)]), woven_in(ratio))
+        b_sum = [keep.tile([P, S], F32, name="b_sum0")]
+        nc.vector.tensor_tensor(b_sum[0][:], b_size[0][:].indirect(n6_t[:]), b_size[1][:, S:], ALU.add)
+        z_codes = keep.tile([P, S], U32, name="z_codes", align_bytes=64)
+        z_plane = keep.tile([P, S], U8, name="z_plane", align_bytes=64)
+        nc.vector.quantize_mx(out=z_codes[:].bitcast(FP8X4), scales=z_plane[:], in_=z_bf16[:])
+        a_banks = product(0, w2, z_codes, z_plane)
+        a_plain = rows4("a_plain")
+        for t in range(PACK):
+            nc.scalar.copy(vals[t][:, :S], a_banks[t][:])
+            nc.sync.dma_start(a_plain[:, t, :], vals[t][:, :S])
+
+        b_sum12 = keep.tile([P, 2, S], F32, name="b_sum12", tag="ratio1")
+        b_sum3 = keep.tile([P, S], F32, name="b_sum3", tag="z_bf16", align_bytes=64)
+        b_sum = [b_sum[0][:], b_sum12[:, 0, :], b_sum12[:, 1, :], b_sum3[:]]
+        for t in range(1, PACK):
+            nc.vector.tensor_tensor(b_sum[t], b_size[t][:].indirect(n6_t[:]), b_size[t ^ 1][:, S:], ALU.add)
+        b_recip = rows4("b_recip")
+        for cols in halves:
+            for t in range(PACK):
+                reciprocal(b_recip[:, t, cols], root[:, t, cols], b_sum[t][:, cols])
+        out_codes = keep.tile([P, S], U32, name="out_codes", align_bytes=64)
+        out_plane = keep.tile([P, S], U8, name="out_plane", align_bytes=64)
+        out_rows = out_0.rearrange("(p t) c -> p t c", t=PACK)
+        out_words = out_1[0].rearrange("p n t -> p (n t)").bitcast(I32)
+        rounded = []
+        for h in range(2):
+            cols = halves[h]
+            diff = keep.tile([P, PACK, HALF], F32, name="diff", tag="diff")
+            result = rows4("result%d" % h, HALF)
+            for t in range(PACK):
+                nc.vector.tensor_tensor(
+                    diff[:, t, :], vals[t][:].indirect(n5_t[:, half_lists[h]]), a_plain[:, t, cols], ALU.subtract
+                )
+            nc.vector.scalar_tensor_tensor(result[:], diff[:], -1.0, b_recip[:, :, cols], ALU.mult, ALU.mult)
+            nc.sync.dma_start(out_rows[:, :, cols], result[:])
+            half = keep.tile([P, PACK * HALF], BF16, name="out_bf16_%d" % h, align_bytes=64)
+            if h == 0:
+                nc.scalar.copy(woven_out(half), woven_in(result))
+            else:
+                nc.vector.tensor_copy(woven_out(half), woven_in(result))
+            rounded.append(half)
+        for h in range(2):
+            cols = halves[h]
+            nc.vector.quantize_mx(out=out_codes[:, cols].bitcast(FP8X4), scales=out_plane[:, cols], in_=rounded[h][:])
+            nc.sync.dma_start(out_words[:, cols], out_codes[:, cols].bitcast(I32))
+        plane_rows = out_2[0].bitcast(I32)
+        for q in range(4):
+            engine = nc.scalar if q % 2 else nc.sync
+            engine.dma_start(plane_rows[4 * q : 4 * q + 4, :], out_plane[32 * q : 32 * q + 4, :].bitcast(I32))

@@ -58,11 +58,11 @@ def tile_picked_forknormbnorm2gmax_none_po_kernel(
         def deal(name, words, plane):
             dealt_words = keep.tile([P, 2 * S], U8, name=name + "_words", align_bytes=64)
             dealt_plane = keep.tile([P, S], U8, name=name + "_plane", align_bytes=64)
-            nc.vector.tensor_copy(
+            nc.gpsimd.tensor_copy(
                 dealt_words[:].rearrange("p (t m b) -> p t m b", t=PACK, b=2),
                 words[:].rearrange("p (m t b) -> p t m b", t=PACK, b=2),
             )
-            nc.vector.tensor_copy(
+            nc.gpsimd.tensor_copy(
                 dealt_plane[:].rearrange("p (t m) -> p t m", t=PACK),
                 plane[:].rearrange("p (m t) -> p t m", t=PACK),
             )
@@ -98,7 +98,7 @@ def tile_picked_forknormbnorm2gmax_none_po_kernel(
             return tile[:].rearrange("p (c i t) -> p c t i", i=4, t=PACK)
 
         def gain_and_quantize(name, values, gain):
-            rounded = keep.tile([P, PACK * S], BF16, name=name + "_bf16", align_bytes=64)
+            rounded = keep.tile([P, PACK * S], BF16, name=name + "_bf16", tag=name + "_bf16", align_bytes=64)
             codes = keep.tile([P, S], U32, name=name + "_codes", align_bytes=64)
             plane = keep.tile([P, S], U8, name=name + "_plane", align_bytes=64)
             spread = gain[:].unsqueeze(1).unsqueeze(3).to_broadcast([P, S // 4, PACK, 4])
@@ -118,21 +118,21 @@ def tile_picked_forknormbnorm2gmax_none_po_kernel(
         halves = [slice(HALF * h, HALF * (h + 1)) for h in range(2)]
         half_lists = [slice(16 * h, 16 * (h + 1)) for h in range(2)]
 
+        xs_raw = zeroed_plane("xs_raw", T, nc.gpsimd)
         w1s_raw = zeroed_plane("w1s_raw", S, nc.gpsimd)
-        xs_raw = zeroed_plane("xs_raw", T, nc.vector)
         offs_t = load_list("offs", offs)
         w1w_raw = load_words("w1w_raw", w1_words)
-        load_plane(w1s_raw, w1_scales, range(1))
+        n4_t = load_list("n4", n4)
+        load_plane(xs_raw, x_scales, range(2))
+        load_plane(xs_raw, x_scales, range(2, 4), nc.scalar)
         xw_raw = keep.tile([P, T], U32, name="xw_raw")
         nc.sync.dma_start(xw_raw[:].bitcast(I32), x_words[0].rearrange("p n t -> p (n t)").bitcast(I32))
-        load_plane(xs_raw, x_scales, range(4), nc.scalar)
-        load_plane(w1s_raw, w1_scales, range(1, 4))
+        load_plane(w1s_raw, w1_scales)
         warm = keep.tile([P, 3], F32, name="warm")
         nc.gpsimd.memset(warm[:, 0:1], 0.0)
         nc.scalar.activation(warm[:, 1:2], warm[:, 0:1], ACT.Sigmoid)
         w3s_raw = zeroed_plane("w3s_raw", S, nc.gpsimd)
         w2s_raw = zeroed_plane("w2s_raw", S, nc.gpsimd)
-        n4_t = load_list("n4", n4)
         w3w_raw = load_words("w3w_raw", w3_words)
         n3_t = load_list("n3", n3)
         load_plane(w3s_raw, w3_scales)
@@ -156,7 +156,9 @@ def tile_picked_forknormbnorm2gmax_none_po_kernel(
         nc.vector.tensor_copy(x_codes[:], xw_raw[:].indirect(offs_t[:]))
         y_banks = product(0, w1, x_codes, x_plane)
         w3 = deal("w3", w3w_raw, w3s_raw)
-        for t in range(PACK):
+        w2 = deal("w2", w2w_raw, w2s_raw)
+        nc.vector.tensor_copy(vals[0][:, :S], y_banks[0][:])
+        for t in range(1, PACK):
             nc.scalar.copy(vals[t][:, :S], y_banks[t][:])
 
         other = rows4("other")
@@ -167,20 +169,20 @@ def tile_picked_forknormbnorm2gmax_none_po_kernel(
             nc.vector.tensor_copy(other[:, t, :], vals[t][:].indirect(n4_t[:]))
         for t in range(PACK):
             nc.scalar.activation(gate[:, t, :], vals[t][:].indirect(n3_t[:]), ACT.Sigmoid)
+        for t in range(PACK):
+            nc.vector.tensor_tensor(gated[:, t, :], gate[:, t, :], y_banks[t][:], ALU.mult)
         y_size = windows("y_size")
         magnitudes(y_size, y_banks)
-        gained = [keep.tile([P, S], F32, name="gained%d" % t) for t in range(PACK)]
+        gained = [keep.tile([P, S], F32, name="gained", tag="gained%d" % t) for t in range(PACK)]
         for t in range(PACK):
             nc.scalar.activation(gained[t][:], y_banks[t][:], ACT.Copy, scale=gn_t[:, t : t + 1])
         nc.scalar.activation(warm[:, 2:3], gate[:, PACK - 1, 0:1], ACT.Abs_reciprocal_sqrt, bias=0.5)
-        for t in range(PACK):
-            nc.vector.tensor_tensor(gated[:, t, :], gate[:, t, :], vals[t][:, :S], ALU.mult)
-        nc.vector.tensor_tensor(larger[:], gated[:], other[:], ALU.max)
+        for pair in (slice(0, 2), slice(2, 4)):
+            nc.vector.tensor_tensor(larger[:, pair, :], gated[:, pair, :], other[:, pair, :], ALU.max)
         z2_codes, z2_plane = gain_and_quantize("z2", larger, gm_t)
         b_banks = product(4, w3, z2_codes, z2_plane)
-        w2 = deal("w2", w2w_raw, w2s_raw)
 
-        y_sum = rows4("y_sum")
+        y_sum = keep.tile([P, PACK, S], F32, name="y_sum", tag="z2_bf16", align_bytes=64)
         root = rows4("root")
         y_recip = rows4("y_recip")
         b_size = windows("b_size")
@@ -192,8 +194,8 @@ def tile_picked_forknormbnorm2gmax_none_po_kernel(
                 for u in (2 * t, 2 * t + 1):
                     nc.scalar.activation(b_size[u][:, :S], b_banks[u][:], ACT.Abs)
                     nc.sync.dma_start(b_size[u ^ 1][:, S:], b_size[u][:, :S])
-        for t in range(PACK):
-            reciprocal(y_recip[:, t, halves[1]], root[:, t, halves[1]], y_sum[:, t, halves[1]])
+        for pair in (slice(0, 2), slice(2, 4)):
+            reciprocal(y_recip[:, pair, halves[1]], root[:, pair, halves[1]], y_sum[:, pair, halves[1]])
         z_bf16 = keep.tile([P, PACK * S], BF16, name="z_bf16", tag="z_bf16", align_bytes=64)
         for h in range(2):
             ratio = keep.tile([P, PACK, HALF], F32, name="ratio", tag="ratio%d" % h)
@@ -202,9 +204,9 @@ def tile_picked_forknormbnorm2gmax_none_po_kernel(
                     ratio[:, t, :], gained[t][:].indirect(n1_t[:, half_lists[h]]), y_recip[:, t, halves[h]], ALU.mult
                 )
             nc.scalar.copy(woven_out(z_bf16[:, PACK * HALF * h : PACK * HALF * (h + 1)]), woven_in(ratio))
-        b_sum = [keep.tile([P, S], F32, name="b_sum0")]
+        b_sum = [keep.tile([P, S], F32, name="b_sum0", tag="gained3")]
         nc.vector.tensor_tensor(b_sum[0][:], b_size[0][:].indirect(n6_t[:]), b_size[1][:, S:], ALU.add)
-        z_codes = keep.tile([P, S], U32, name="z_codes", align_bytes=64)
+        z_codes = keep.tile([P, S], U32, name="z_codes", tag="z_codes", align_bytes=64)
         z_plane = keep.tile([P, S], U8, name="z_plane", align_bytes=64)
         nc.vector.quantize_mx(out=z_codes[:].bitcast(FP8X4), scales=z_plane[:], in_=z_bf16[:])
         a_banks = product(0, w2, z_codes, z_plane)
@@ -219,9 +221,10 @@ def tile_picked_forknormbnorm2gmax_none_po_kernel(
         for t in range(1, PACK):
             nc.vector.tensor_tensor(b_sum[t], b_size[t][:].indirect(n6_t[:]), b_size[t ^ 1][:, S:], ALU.add)
         b_recip = rows4("b_recip")
+        b_root = keep.tile([P, PACK, S], F32, name="b_root", tag="z_codes", align_bytes=64)
         for cols in halves:
             for t in range(PACK):
-                reciprocal(b_recip[:, t, cols], root[:, t, cols], b_sum[t][:, cols])
+                reciprocal(b_recip[:, t, cols], (b_root if t else root)[:, t, cols], b_sum[t][:, cols])
         out_codes = keep.tile([P, S], U32, name="out_codes", align_bytes=64)
         out_plane = keep.tile([P, S], U8, name="out_plane", align_bytes=64)
         out_rows = out_0.rearrange("(p t) c -> p t c", t=PACK)

@@ -68,20 +68,23 @@ def tile_picked_forknormbnorm2gmax_none_po_kernel(
             )
             return dealt_words, dealt_plane
 
-        def product(first_bank, weights, codes, plane):
+        def one_pass(out, weights, t, codes, plane):
             words, scales = weights
+            nc.tensor.matmul_mx(
+                out=out,
+                lhsT=words[:, 2 * P * t : 2 * P * (t + 1)].bitcast(FP4X4),
+                lhsT_scale=scales[:, P * t : P * (t + 1)],
+                rhs=codes.bitcast(FP8X4),
+                rhs_scale=plane,
+                start=True,
+                stop=True,
+            )
+
+        def product(first_bank, weights, codes, plane):
             banks = []
             for t in range(PACK):
                 bank = psum.tile([P, S], F32, name="bank", tag="bank%d" % (first_bank + t))
-                nc.tensor.matmul_mx(
-                    out=bank[:],
-                    lhsT=words[:, 2 * P * t : 2 * P * (t + 1)].bitcast(FP4X4),
-                    lhsT_scale=scales[:, P * t : P * (t + 1)],
-                    rhs=codes[:].bitcast(FP8X4),
-                    rhs_scale=plane[:],
-                    start=True,
-                    stop=True,
-                )
+                one_pass(bank[:], weights, t, codes[:], plane[:])
                 banks.append(bank)
             return banks
 
@@ -106,9 +109,9 @@ def tile_picked_forknormbnorm2gmax_none_po_kernel(
             nc.vector.quantize_mx(out=codes[:].bitcast(FP8X4), scales=plane[:], in_=rounded[:])
             return codes, plane
 
-        def magnitudes(wins, banks):
-            for t in range(PACK):
-                nc.scalar.activation(wins[t][:, :S], banks[t][:], ACT.Abs)
+        def magnitudes(wins, banks, tiles):
+            for t in tiles:
+                nc.scalar.activation(wins[t][:, :S], banks[t][:, :S], ACT.Abs)
                 nc.sync.dma_start(wins[t ^ 1][:, S:], wins[t][:, :S])
 
         def reciprocal(recip, root, total):
@@ -118,8 +121,10 @@ def tile_picked_forknormbnorm2gmax_none_po_kernel(
         halves = [slice(HALF * h, HALF * (h + 1)) for h in range(2)]
         half_lists = [slice(16 * h, 16 * (h + 1)) for h in range(2)]
 
-        xs_raw = zeroed_plane("xs_raw", T, nc.gpsimd)
-        w1s_raw = zeroed_plane("w1s_raw", S, nc.gpsimd)
+        xs_raw = keep.tile([P, T], U8, name="xs_raw", tag="xs_raw", align_bytes=64)
+        nc.vector.memset(xs_raw[:, : T // 2].bitcast(I32), 0)
+        nc.gpsimd.memset(xs_raw[:, T // 2 :].bitcast(I32), 0)
+        w1s_raw = zeroed_plane("w1s_raw", S, nc.vector)
         offs_t = load_list("offs", offs)
         w1w_raw = load_words("w1w_raw", w1_words)
         n4_t = load_list("n4", n4)
@@ -136,30 +141,37 @@ def tile_picked_forknormbnorm2gmax_none_po_kernel(
         w3w_raw = load_words("w3w_raw", w3_words)
         n3_t = load_list("n3", n3)
         load_plane(w3s_raw, w3_scales)
-        gm_t = load_gain("gm", gm)
+        gn_t = load_gain("gn", gn)
         w2w_raw = load_words("w2w_raw", w2_words)
         load_plane(w2s_raw, w2_scales)
-        gn_t = load_gain("gn", gn)
+        gm_t = load_gain("gm", gm)
         n2_t = load_list("n2", n2)
         n1_t = load_list("n1", n1)
         n6_t = load_list("n6", n6)
         n5_t = load_list("n5", n5)
 
         vals = windows("vals")
-        for t in range(PACK):
-            nc.vector.memset(vals[t][:, S:], 0.0)
+        nc.vector.memset(vals[0][:, S:], 0.0)
+        for t in range(1, PACK):
+            nc.scalar.copy(vals[t][:, S:], vals[0][:, S:])
 
         w1 = deal("w1", w1w_raw, w1s_raw)
         x_plane = keep.tile([P, S], U8, name="x_plane", align_bytes=64)
         nc.vector.tensor_copy(x_plane[:], xs_raw[:].indirect(offs_t[:]))
         x_codes = keep.tile([P, S], U32, name="x_codes", tag="xs_raw", align_bytes=64)
-        nc.vector.tensor_copy(x_codes[:], xw_raw[:].indirect(offs_t[:]))
-        y_banks = product(0, w1, x_codes, x_plane)
+        for h in range(2):
+            nc.vector.tensor_copy(x_codes[:, halves[h]], xw_raw[:].indirect(offs_t[:, half_lists[h]]))
+        pieces = [(t, cols) for cols in halves for t in (0, 1)] + [(t, slice(0, S)) for t in (2, 3)]
+        y_pieces = []
+        for n, (t, cols) in enumerate(pieces):
+            bank = psum.tile([P, cols.stop - cols.start], F32, name="bank", tag="bank%d" % n)
+            one_pass(bank[:], w1, t, x_codes[:, cols], x_plane[:, cols])
+            if n < 3:
+                nc.vector.tensor_copy(vals[t][:, cols], bank[:])
+            else:
+                nc.scalar.copy(vals[t][:, cols], bank[:])
+            y_pieces.append((t, cols, bank))
         w3 = deal("w3", w3w_raw, w3s_raw)
-        w2 = deal("w2", w2w_raw, w2s_raw)
-        nc.vector.tensor_copy(vals[0][:, :S], y_banks[0][:])
-        for t in range(1, PACK):
-            nc.scalar.copy(vals[t][:, :S], y_banks[t][:])
 
         other = rows4("other")
         gate = rows4("gate")
@@ -167,35 +179,46 @@ def tile_picked_forknormbnorm2gmax_none_po_kernel(
         larger = rows4("larger")
         for t in range(PACK):
             nc.vector.tensor_copy(other[:, t, :], vals[t][:].indirect(n4_t[:]))
+        y_size = windows("y_size")
+        magnitudes(y_size, vals, (0, 1))
         for t in range(PACK):
             nc.scalar.activation(gate[:, t, :], vals[t][:].indirect(n3_t[:]), ACT.Sigmoid)
-        for t in range(PACK):
-            nc.vector.tensor_tensor(gated[:, t, :], gate[:, t, :], y_banks[t][:], ALU.mult)
-        y_size = windows("y_size")
-        magnitudes(y_size, y_banks)
+        for t in range(PACK + 1):
+            for u, cols, bank in y_pieces:
+                if u == t:
+                    nc.vector.tensor_tensor(gated[:, t, cols], gate[:, t, cols], bank[:], ALU.mult)
+            if t:
+                nc.vector.tensor_tensor(larger[:, t - 1, :], gated[:, t - 1, :], other[:, t - 1, :], ALU.max)
+        magnitudes(y_size, vals, (2, 3))
         gained = [keep.tile([P, S], F32, name="gained", tag="gained%d" % t) for t in range(PACK)]
         for t in range(PACK):
-            nc.scalar.activation(gained[t][:], y_banks[t][:], ACT.Copy, scale=gn_t[:, t : t + 1])
-        nc.scalar.activation(warm[:, 2:3], gate[:, PACK - 1, 0:1], ACT.Abs_reciprocal_sqrt, bias=0.5)
-        for pair in (slice(0, 2), slice(2, 4)):
-            nc.vector.tensor_tensor(larger[:, pair, :], gated[:, pair, :], other[:, pair, :], ALU.max)
-        z2_codes, z2_plane = gain_and_quantize("z2", larger, gm_t)
+            nc.gpsimd.tensor_scalar(gained[t][:], vals[t][:, :S], gn_t[:, t : t + 1], 0.0, ALU.mult, ALU.add)
+        w2 = deal("w2", w2w_raw, w2s_raw)
+        nc.scalar.activation(warm[:, 2:3], y_size[PACK - 1][:, 0:1], ACT.Abs_reciprocal_sqrt, bias=0.5)
+        y_sum = keep.tile([P, PACK + 1, S], F32, name="y_sum")
+        z2_rows = y_sum[:, PACK - 1 :, :].rearrange("p a c -> p (a c)").bitcast(BF16).rearrange("p (t c) -> p t c", t=PACK)
+        for t in range(PACK):
+            nc.scalar.activation(z2_rows[:, t, :], larger[:, t, :], ACT.Copy, scale=gm_t[:, t : t + 1])
+        z2_bf16 = keep.tile([P, PACK * S], BF16, name="z2_bf16", align_bytes=64)
+        z2_codes = keep.tile([P, S], U32, name="z2_codes", align_bytes=64)
+        z2_plane = keep.tile([P, S], U8, name="z2_plane", align_bytes=64)
+        for t in range(PACK):
+            if t == PACK - 1:
+                nc.vector.tensor_copy(woven_out(z2_bf16), woven_in(z2_rows))
+                nc.vector.quantize_mx(out=z2_codes[:].bitcast(FP8X4), scales=z2_plane[:], in_=z2_bf16[:])
+            nc.vector.tensor_tensor(y_sum[:, t, :], y_size[t][:].indirect(n2_t[:]), y_size[t ^ 1][:, S:], ALU.add)
         b_banks = product(4, w3, z2_codes, z2_plane)
 
-        y_sum = keep.tile([P, PACK, S], F32, name="y_sum", tag="z2_bf16", align_bytes=64)
         root = rows4("root")
         y_recip = rows4("y_recip")
         b_size = windows("b_size")
         for t in range(PACK):
-            nc.vector.tensor_tensor(y_sum[:, t, :], y_size[t][:].indirect(n2_t[:]), y_size[t ^ 1][:, S:], ALU.add)
-        for t in range(PACK):
+            if t == PACK - 1:
+                magnitudes(b_size, b_banks, (0, 1))
             reciprocal(y_recip[:, t, halves[0]], root[:, t, halves[0]], y_sum[:, t, halves[0]])
-            if t < 2:
-                for u in (2 * t, 2 * t + 1):
-                    nc.scalar.activation(b_size[u][:, :S], b_banks[u][:], ACT.Abs)
-                    nc.sync.dma_start(b_size[u ^ 1][:, S:], b_size[u][:, :S])
         for pair in (slice(0, 2), slice(2, 4)):
             reciprocal(y_recip[:, pair, halves[1]], root[:, pair, halves[1]], y_sum[:, pair, halves[1]])
+        magnitudes(b_size, b_banks, (2, 3))
         z_bf16 = keep.tile([P, PACK * S], BF16, name="z_bf16", tag="z_bf16", align_bytes=64)
         for h in range(2):
             ratio = keep.tile([P, PACK, HALF], F32, name="ratio", tag="ratio%d" % h)
@@ -204,16 +227,24 @@ def tile_picked_forknormbnorm2gmax_none_po_kernel(
                     ratio[:, t, :], gained[t][:].indirect(n1_t[:, half_lists[h]]), y_recip[:, t, halves[h]], ALU.mult
                 )
             nc.scalar.copy(woven_out(z_bf16[:, PACK * HALF * h : PACK * HALF * (h + 1)]), woven_in(ratio))
-        b_sum = [keep.tile([P, S], F32, name="b_sum0", tag="gained3")]
-        nc.vector.tensor_tensor(b_sum[0][:], b_size[0][:].indirect(n6_t[:]), b_size[1][:, S:], ALU.add)
         z_codes = keep.tile([P, S], U32, name="z_codes", tag="z_codes", align_bytes=64)
         z_plane = keep.tile([P, S], U8, name="z_plane", align_bytes=64)
-        nc.vector.quantize_mx(out=z_codes[:].bitcast(FP8X4), scales=z_plane[:], in_=z_bf16[:])
-        a_banks = product(0, w2, z_codes, z_plane)
+        a_banks = [psum.tile([P, S], F32, name="bank", tag="bank%d" % t) for t in range(PACK)]
         a_plain = rows4("a_plain")
-        for t in range(PACK):
-            nc.scalar.copy(vals[t][:, :S], a_banks[t][:])
-            nc.sync.dma_start(a_plain[:, t, :], vals[t][:, :S])
+        b_sum = [keep.tile([P, S], F32, name="b_sum0", tag="gained3")]
+        for h in range(2):
+            cols = halves[h]
+            if h == 1:
+                nc.vector.tensor_tensor(b_sum[0][:], b_size[0][:].indirect(n6_t[:]), b_size[1][:, S:], ALU.add)
+            nc.vector.quantize_mx(
+                out=z_codes[:, cols].bitcast(FP8X4),
+                scales=z_plane[:, cols],
+                in_=z_bf16[:, PACK * cols.start : PACK * cols.stop],
+            )
+            for t in range(PACK):
+                one_pass(a_banks[t][:, cols], w2, t, z_codes[:, cols], z_plane[:, cols])
+                nc.scalar.copy(vals[t][:, cols], a_banks[t][:, cols])
+                nc.sync.dma_start(a_plain[:, t, cols], vals[t][:, cols])
 
         b_sum12 = keep.tile([P, 2, S], F32, name="b_sum12", tag="ratio1")
         b_sum3 = keep.tile([P, S], F32, name="b_sum3", tag="z_bf16", align_bytes=64)

@@ -14,10 +14,12 @@ ACT = mybir.ActivationFunctionType
 ALU = mybir.AluOpType
 
 P = 128
-PACK = 4
+SLABS = 4
+QUADRANTS = 4
 T = 2048
 S = 512
 HALF = S // 2
+LINE = 4
 FLOPS = 3 * 2 * 512 * 512 * 512
 
 
@@ -26,6 +28,9 @@ def tile_picked_forknormbnorm2gmax_none_po_kernel(
     offs, n1, n2, n3, n4, n5, n6, out_0, out_1, out_2,
 ):
     nc = tc.nc
+    halves = [slice(HALF * h, HALF * (h + 1)) for h in range(2)]
+    list_halves = [slice(HALF // 16 * h, HALF // 16 * (h + 1)) for h in range(2)]
+
     with ExitStack() as ctx:
         keep = ctx.enter_context(tc.tile_pool(name="keep", bufs=1))
         psum = ctx.enter_context(tc.psum_pool(name="psum", bufs=1))
@@ -35,12 +40,12 @@ def tile_picked_forknormbnorm2gmax_none_po_kernel(
             nc.sync.dma_start(tile[:], src)
             return tile
 
-        def zeroed_plane(name, width, engine):
-            tile = keep.tile([P, width], U8, name=name, tag=name, align_bytes=64)
+        def zeroed_plane(name, engine):
+            tile = keep.tile([P, S], U8, name=name, align_bytes=64)
             engine.memset(tile[:].bitcast(I32), 0)
             return tile
 
-        def load_plane(tile, src, quadrants=range(4), engine=nc.sync):
+        def load_plane(tile, src, quadrants, engine):
             rows = src[0].bitcast(I32)
             for q in quadrants:
                 engine.dma_start(tile[32 * q : 32 * q + 4, :].bitcast(I32), rows[4 * q : 4 * q + 4, :])
@@ -51,25 +56,28 @@ def tile_picked_forknormbnorm2gmax_none_po_kernel(
             return tile
 
         def load_gain(name, src):
-            tile = keep.tile([P, PACK], F32, name=name)
-            nc.sync.dma_start(tile[:], src.rearrange("(p t) o -> p (t o)", t=PACK))
+            tile = keep.tile([P, SLABS], F32, name=name)
+            nc.sync.dma_start(tile[:], src.rearrange("(p t) o -> p (t o)", t=SLABS))
             return tile
 
         def deal(name, words, plane):
             dealt_words = keep.tile([P, 2 * S], U8, name=name + "_words", align_bytes=64)
             dealt_plane = keep.tile([P, S], U8, name=name + "_plane", align_bytes=64)
             nc.gpsimd.tensor_copy(
-                dealt_words[:].rearrange("p (t m b) -> p t m b", t=PACK, b=2),
-                words[:].rearrange("p (m t b) -> p t m b", t=PACK, b=2),
+                dealt_words[:].rearrange("p (t m b) -> p t m b", t=SLABS, b=2),
+                words[:].rearrange("p (m t b) -> p t m b", t=SLABS, b=2),
             )
             nc.gpsimd.tensor_copy(
-                dealt_plane[:].rearrange("p (t m) -> p t m", t=PACK),
-                plane[:].rearrange("p (m t) -> p t m", t=PACK),
+                dealt_plane[:].rearrange("p (t m) -> p t m", t=SLABS),
+                plane[:].rearrange("p (m t) -> p t m", t=SLABS),
             )
             return dealt_words, dealt_plane
 
-        def one_pass(out, weights, t, codes, plane):
-            words, scales = weights
+        def bank(number, width=S):
+            return psum.tile([P, width], F32, name="bank", tag="bank%d" % number)
+
+        def slab_product(out, weight, t, codes, plane):
+            words, scales = weight
             nc.tensor.matmul_mx(
                 out=out,
                 lhsT=words[:, 2 * P * t : 2 * P * (t + 1)].bitcast(FP4X4),
@@ -80,208 +88,198 @@ def tile_picked_forknormbnorm2gmax_none_po_kernel(
                 stop=True,
             )
 
-        def product(first_bank, weights, codes, plane):
-            banks = []
-            for t in range(PACK):
-                bank = psum.tile([P, S], F32, name="bank", tag="bank%d" % (first_bank + t))
-                one_pass(bank[:], weights, t, codes[:], plane[:])
-                banks.append(bank)
-            return banks
-
-        def rows4(name, width=S):
-            return keep.tile([P, PACK, width], F32, name=name)
+        def slabs(name, width=S, tag=None):
+            return keep.tile([P, SLABS, width], F32, name=name, tag=tag or name)
 
         def windows(name):
-            return [keep.tile([P, 2 * S], F32, name="%s%d" % (name, t)) for t in range(PACK)]
+            return [
+                keep.tile([P, 2 * S], F32, name=name, tag="%s%d" % (name, t), align_bytes=64) for t in range(SLABS)
+            ]
 
-        def woven_in(tile):
-            return tile[:].rearrange("p t (c i) -> p c t i", i=4)
+        def weave(copy, woven, values):
+            copy(
+                woven.rearrange("p (c i t) -> p c t i", i=LINE, t=SLABS),
+                values.rearrange("p t (c i) -> p c t i", i=LINE),
+            )
 
-        def woven_out(tile):
-            return tile[:].rearrange("p (c i t) -> p c t i", i=4, t=PACK)
+        def sizes(size, values, which):
+            for t in which:
+                nc.scalar.activation(size[t][:, :S], values[t][:, :S], ACT.Abs)
+                nc.sync.dma_start(size[t ^ 1][:, S:], size[t][:, :S])
 
-        def gain_and_quantize(name, values, gain):
-            rounded = keep.tile([P, PACK * S], BF16, name=name + "_bf16", tag=name + "_bf16", align_bytes=64)
-            codes = keep.tile([P, S], U32, name=name + "_codes", align_bytes=64)
-            plane = keep.tile([P, S], U8, name=name + "_plane", align_bytes=64)
-            spread = gain[:].unsqueeze(1).unsqueeze(3).to_broadcast([P, S // 4, PACK, 4])
-            nc.vector.tensor_tensor(woven_out(rounded), woven_in(values), spread, ALU.mult)
-            nc.vector.quantize_mx(out=codes[:].bitcast(FP8X4), scales=plane[:], in_=rounded[:])
-            return codes, plane
+        def add_looked_up_size(out, size, t, places):
+            nc.vector.tensor_tensor(out, size[t][:].indirect(places[:]), size[t ^ 1][:, S:], ALU.add)
 
-        def magnitudes(wins, banks, tiles):
-            for t in tiles:
-                nc.scalar.activation(wins[t][:, :S], banks[t][:, :S], ACT.Abs)
-                nc.sync.dma_start(wins[t ^ 1][:, S:], wins[t][:, :S])
-
-        def reciprocal(recip, root, total):
+        def reciprocal(out, root, total):
             nc.scalar.activation(root, total, ACT.Abs_reciprocal_sqrt, bias=0.5)
-            nc.scalar.activation(recip, root, ACT.Square)
+            nc.scalar.activation(out, root, ACT.Square)
 
-        halves = [slice(HALF * h, HALF * (h + 1)) for h in range(2)]
-        half_lists = [slice(16 * h, 16 * (h + 1)) for h in range(2)]
+        x_plane_all = keep.tile([P, T], U8, name="x_plane_all", tag="x_plane_all", align_bytes=64)
+        nc.vector.memset(x_plane_all[:, : T // 2].bitcast(I32), 0)
+        nc.gpsimd.memset(x_plane_all[:, T // 2 :].bitcast(I32), 0)
+        w1_plane = zeroed_plane("w1_plane_loaded", nc.vector)
+        offs_list = load_list("offs", offs)
+        w1_codes = load_words("w1_codes_loaded", w1_words)
+        n4_list = load_list("n4", n4)
+        load_plane(x_plane_all, x_scales, range(QUADRANTS // 2), nc.sync)
+        load_plane(x_plane_all, x_scales, range(QUADRANTS // 2, QUADRANTS), nc.scalar)
+        x_codes_all = keep.tile([P, T], U32, name="x_codes_all")
+        nc.sync.dma_start(x_codes_all[:].bitcast(I32), x_words[0].rearrange("p n t -> p (n t)").bitcast(I32))
+        load_plane(w1_plane, w1_scales, range(QUADRANTS), nc.sync)
+        w3_plane = zeroed_plane("w3_plane_loaded", nc.gpsimd)
+        w2_plane = zeroed_plane("w2_plane_loaded", nc.gpsimd)
+        w3_codes = load_words("w3_codes_loaded", w3_words)
+        n3_list = load_list("n3", n3)
+        load_plane(w3_plane, w3_scales, range(QUADRANTS), nc.sync)
+        gn_slabs = load_gain("gn", gn)
+        w2_codes = load_words("w2_codes_loaded", w2_words)
+        load_plane(w2_plane, w2_scales, range(QUADRANTS), nc.sync)
+        gm_slabs = load_gain("gm", gm)
+        n2_list = load_list("n2", n2)
+        n1_list = load_list("n1", n1)
+        n6_list = load_list("n6", n6)
+        n5_list = load_list("n5", n5)
 
-        xs_raw = keep.tile([P, T], U8, name="xs_raw", tag="xs_raw", align_bytes=64)
-        nc.vector.memset(xs_raw[:, : T // 2].bitcast(I32), 0)
-        nc.gpsimd.memset(xs_raw[:, T // 2 :].bitcast(I32), 0)
-        w1s_raw = zeroed_plane("w1s_raw", S, nc.vector)
-        offs_t = load_list("offs", offs)
-        w1w_raw = load_words("w1w_raw", w1_words)
-        n4_t = load_list("n4", n4)
-        load_plane(xs_raw, x_scales, range(2))
-        load_plane(xs_raw, x_scales, range(2, 4), nc.scalar)
-        xw_raw = keep.tile([P, T], U32, name="xw_raw")
-        nc.sync.dma_start(xw_raw[:].bitcast(I32), x_words[0].rearrange("p n t -> p (n t)").bitcast(I32))
-        load_plane(w1s_raw, w1_scales)
-        warm = keep.tile([P, 3], F32, name="warm")
-        nc.gpsimd.memset(warm[:, 0:1], 0.0)
-        nc.scalar.activation(warm[:, 1:2], warm[:, 0:1], ACT.Sigmoid)
-        w3s_raw = zeroed_plane("w3s_raw", S, nc.gpsimd)
-        w2s_raw = zeroed_plane("w2s_raw", S, nc.gpsimd)
-        w3w_raw = load_words("w3w_raw", w3_words)
-        n3_t = load_list("n3", n3)
-        load_plane(w3s_raw, w3_scales)
-        gn_t = load_gain("gn", gn)
-        w2w_raw = load_words("w2w_raw", w2_words)
-        load_plane(w2s_raw, w2_scales)
-        gm_t = load_gain("gm", gm)
-        n2_t = load_list("n2", n2)
-        n1_t = load_list("n1", n1)
-        n6_t = load_list("n6", n6)
-        n5_t = load_list("n5", n5)
+        result_windows = windows("result_window")
+        nc.vector.memset(result_windows[0][:, S:], 0.0)
+        for t in range(1, SLABS):
+            nc.scalar.activation(result_windows[t][:, S:], result_windows[0][:, S:], ACT.Sigmoid)
 
-        vals = windows("vals")
-        nc.vector.memset(vals[0][:, S:], 0.0)
-        for t in range(1, PACK):
-            nc.scalar.copy(vals[t][:, S:], vals[0][:, S:])
-
-        w1 = deal("w1", w1w_raw, w1s_raw)
+        w1 = deal("w1", w1_codes, w1_plane)
         x_plane = keep.tile([P, S], U8, name="x_plane", align_bytes=64)
-        nc.vector.tensor_copy(x_plane[:], xs_raw[:].indirect(offs_t[:]))
-        x_codes = keep.tile([P, S], U32, name="x_codes", tag="xs_raw", align_bytes=64)
+        nc.vector.tensor_copy(x_plane[:], x_plane_all[:].indirect(offs_list[:]))
+        x_codes = keep.tile([P, S], U32, name="x_codes", tag="x_plane_all", align_bytes=64)
         for h in range(2):
-            nc.vector.tensor_copy(x_codes[:, halves[h]], xw_raw[:].indirect(offs_t[:, half_lists[h]]))
+            nc.vector.tensor_copy(x_codes[:, halves[h]], x_codes_all[:].indirect(offs_list[:, list_halves[h]]))
         pieces = [(t, cols) for cols in halves for t in (0, 1)] + [(t, slice(0, S)) for t in (2, 3)]
+        last_piece_of_slab_0 = pieces.index((0, halves[1]))
         y_pieces = []
-        for n, (t, cols) in enumerate(pieces):
-            bank = psum.tile([P, cols.stop - cols.start], F32, name="bank", tag="bank%d" % n)
-            one_pass(bank[:], w1, t, x_codes[:, cols], x_plane[:, cols])
-            if n < 3:
-                nc.vector.tensor_copy(vals[t][:, cols], bank[:])
-            else:
-                nc.scalar.copy(vals[t][:, cols], bank[:])
-            y_pieces.append((t, cols, bank))
-        w3 = deal("w3", w3w_raw, w3s_raw)
+        for number, (t, cols) in enumerate(pieces):
+            y_bank = bank(number, cols.stop - cols.start)
+            slab_product(y_bank[:], w1, t, x_codes[:, cols], x_plane[:, cols])
+            copy = nc.vector.tensor_copy if number <= last_piece_of_slab_0 else nc.scalar.copy
+            copy(result_windows[t][:, cols], y_bank[:])
+            y_pieces.append((t, cols, y_bank))
+        w3 = deal("w3", w3_codes, w3_plane)
 
-        other = rows4("other")
-        gate = rows4("gate")
-        gated = rows4("gated")
-        larger = rows4("larger")
-        for t in range(PACK):
-            nc.vector.tensor_copy(other[:, t, :], vals[t][:].indirect(n4_t[:]))
+        y_n4 = slabs("y_n4")
+        gate = slabs("gate")
+        gated = slabs("gated")
+        larger = slabs("larger")
+        for t in range(SLABS):
+            nc.vector.tensor_copy(y_n4[:, t, :], result_windows[t][:].indirect(n4_list[:]))
         y_size = windows("y_size")
-        magnitudes(y_size, vals, (0, 1))
-        for t in range(PACK):
-            nc.scalar.activation(gate[:, t, :], vals[t][:].indirect(n3_t[:]), ACT.Sigmoid)
-        for t in range(PACK + 1):
-            for u, cols, bank in y_pieces:
-                if u == t:
-                    nc.vector.tensor_tensor(gated[:, t, cols], gate[:, t, cols], bank[:], ALU.mult)
+        sizes(y_size, result_windows, (0, 1))
+        for t in range(SLABS):
+            nc.scalar.activation(gate[:, t, :], result_windows[t][:].indirect(n3_list[:]), ACT.Sigmoid)
+        for t in range(SLABS + 1):
+            for slab, cols, y_bank in y_pieces:
+                if slab == t:
+                    nc.vector.tensor_tensor(gated[:, t, cols], gate[:, t, cols], y_bank[:], ALU.mult)
             if t:
-                nc.vector.tensor_tensor(larger[:, t - 1, :], gated[:, t - 1, :], other[:, t - 1, :], ALU.max)
-        magnitudes(y_size, vals, (2, 3))
-        gained = [keep.tile([P, S], F32, name="gained", tag="gained%d" % t) for t in range(PACK)]
-        for t in range(PACK):
-            nc.gpsimd.tensor_scalar(gained[t][:], vals[t][:, :S], gn_t[:, t : t + 1], 0.0, ALU.mult, ALU.add)
-        w2 = deal("w2", w2w_raw, w2s_raw)
-        nc.scalar.activation(warm[:, 2:3], y_size[PACK - 1][:, 0:1], ACT.Abs_reciprocal_sqrt, bias=0.5)
-        y_sum = keep.tile([P, PACK + 1, S], F32, name="y_sum")
-        z2_rows = y_sum[:, PACK - 1 :, :].rearrange("p a c -> p (a c)").bitcast(BF16).rearrange("p (t c) -> p t c", t=PACK)
-        for t in range(PACK):
-            nc.scalar.activation(z2_rows[:, t, :], larger[:, t, :], ACT.Copy, scale=gm_t[:, t : t + 1])
-        z2_bf16 = keep.tile([P, PACK * S], BF16, name="z2_bf16", align_bytes=64)
+                nc.vector.tensor_tensor(larger[:, t - 1, :], gated[:, t - 1, :], y_n4[:, t - 1, :], ALU.max)
+        sizes(y_size, result_windows, (2, 3))
+        y_gained = [keep.tile([P, S], F32, name="y_gained", tag="y_gained%d" % t) for t in range(SLABS)]
+        for t in range(SLABS):
+            nc.gpsimd.tensor_scalar(
+                y_gained[t][:], result_windows[t][:, :S], gn_slabs[:, t : t + 1], 0.0, ALU.mult, ALU.add
+            )
+        w2 = deal("w2", w2_codes, w2_plane)
+        y_total = [keep.tile([P, S], F32, name="y_total%d" % t) for t in range(SLABS)]
+        z2_slabs = keep.tile([P, SLABS, S], BF16, name="z2_slabs")
+        for t in range(SLABS):
+            nc.scalar.activation(z2_slabs[:, t, :], larger[:, t, :], ACT.Copy, scale=gm_slabs[:, t : t + 1])
         z2_codes = keep.tile([P, S], U32, name="z2_codes", align_bytes=64)
         z2_plane = keep.tile([P, S], U8, name="z2_plane", align_bytes=64)
-        for t in range(PACK):
-            if t == PACK - 1:
-                nc.vector.tensor_copy(woven_out(z2_bf16), woven_in(z2_rows))
-                nc.vector.quantize_mx(out=z2_codes[:].bitcast(FP8X4), scales=z2_plane[:], in_=z2_bf16[:])
-            nc.vector.tensor_tensor(y_sum[:, t, :], y_size[t][:].indirect(n2_t[:]), y_size[t ^ 1][:, S:], ALU.add)
-        b_banks = product(4, w3, z2_codes, z2_plane)
 
-        root = rows4("root")
-        y_recip = rows4("y_recip")
+        for t in (0, 1):
+            add_looked_up_size(y_total[t][:], y_size, t, n2_list)
+        z2_woven = keep.tile([P, SLABS * S], BF16, name="z2_woven", tag="y_size0", align_bytes=64)
+        weave(nc.vector.tensor_copy, z2_woven[:], z2_slabs[:])
+        nc.vector.quantize_mx(out=z2_codes[:].bitcast(FP8X4), scales=z2_plane[:], in_=z2_woven[:])
+        for t in (2, 3):
+            add_looked_up_size(y_total[t][:], y_size, t, n2_list)
+
+        b_banks = [bank(SLABS + t) for t in range(SLABS)]
+        for t in range(SLABS):
+            slab_product(b_banks[t][:], w3, t, z2_codes[:], z2_plane[:])
+
+        y_root = slabs("y_root", tag="z_half1")
+        y_recip = slabs("y_recip")
         b_size = windows("b_size")
-        for t in range(PACK):
-            if t == PACK - 1:
-                magnitudes(b_size, b_banks, (0, 1))
-            reciprocal(y_recip[:, t, halves[0]], root[:, t, halves[0]], y_sum[:, t, halves[0]])
-        for pair in (slice(0, 2), slice(2, 4)):
-            reciprocal(y_recip[:, pair, halves[1]], root[:, pair, halves[1]], y_sum[:, pair, halves[1]])
-        magnitudes(b_size, b_banks, (2, 3))
-        z_bf16 = keep.tile([P, PACK * S], BF16, name="z_bf16", tag="z_bf16", align_bytes=64)
+        for t in range(SLABS):
+            reciprocal(y_recip[:, t, :], y_root[:, t, :], y_total[t][:])
+        sizes(b_size, b_banks, range(SLABS))
+        z_woven = keep.tile([P, SLABS * S], BF16, name="z_woven", tag="z_woven", align_bytes=64)
+        woven_halves = [slice(SLABS * cols.start, SLABS * cols.stop) for cols in halves]
         for h in range(2):
-            ratio = keep.tile([P, PACK, HALF], F32, name="ratio", tag="ratio%d" % h)
-            for t in range(PACK):
+            z_half = slabs("z_half", HALF, tag="z_half%d" % h)
+            for t in range(SLABS):
                 nc.vector.tensor_tensor(
-                    ratio[:, t, :], gained[t][:].indirect(n1_t[:, half_lists[h]]), y_recip[:, t, halves[h]], ALU.mult
+                    z_half[:, t, :],
+                    y_gained[t][:].indirect(n1_list[:, list_halves[h]]),
+                    y_recip[:, t, halves[h]],
+                    ALU.mult,
                 )
-            nc.scalar.copy(woven_out(z_bf16[:, PACK * HALF * h : PACK * HALF * (h + 1)]), woven_in(ratio))
+            weave(nc.scalar.copy, z_woven[:, woven_halves[h]], z_half[:])
+
         z_codes = keep.tile([P, S], U32, name="z_codes", tag="z_codes", align_bytes=64)
         z_plane = keep.tile([P, S], U8, name="z_plane", align_bytes=64)
-        a_banks = [psum.tile([P, S], F32, name="bank", tag="bank%d" % t) for t in range(PACK)]
-        a_plain = rows4("a_plain")
-        b_sum = [keep.tile([P, S], F32, name="b_sum0", tag="gained3")]
-        for h in range(2):
-            cols = halves[h]
-            if h == 1:
-                nc.vector.tensor_tensor(b_sum[0][:], b_size[0][:].indirect(n6_t[:]), b_size[1][:, S:], ALU.add)
-            nc.vector.quantize_mx(
-                out=z_codes[:, cols].bitcast(FP8X4),
-                scales=z_plane[:, cols],
-                in_=z_bf16[:, PACK * cols.start : PACK * cols.stop],
-            )
-            for t in range(PACK):
-                one_pass(a_banks[t][:, cols], w2, t, z_codes[:, cols], z_plane[:, cols])
-                nc.scalar.copy(vals[t][:, cols], a_banks[t][:, cols])
-                nc.sync.dma_start(a_plain[:, t, cols], vals[t][:, cols])
+        a_banks = [bank(t) for t in range(SLABS)]
+        a_plain = slabs("a_plain")
 
-        b_sum12 = keep.tile([P, 2, S], F32, name="b_sum12", tag="ratio1")
-        b_sum3 = keep.tile([P, S], F32, name="b_sum3", tag="z_bf16", align_bytes=64)
-        b_sum = [b_sum[0][:], b_sum12[:, 0, :], b_sum12[:, 1, :], b_sum3[:]]
-        for t in range(1, PACK):
-            nc.vector.tensor_tensor(b_sum[t], b_size[t][:].indirect(n6_t[:]), b_size[t ^ 1][:, S:], ALU.add)
-        b_recip = rows4("b_recip")
-        b_root = keep.tile([P, PACK, S], F32, name="b_root", tag="z_codes", align_bytes=64)
+        def half_of_a(h):
+            cols = halves[h]
+            nc.vector.quantize_mx(
+                out=z_codes[:, cols].bitcast(FP8X4), scales=z_plane[:, cols], in_=z_woven[:, woven_halves[h]]
+            )
+            for t in range(SLABS):
+                slab_product(a_banks[t][:, cols], w2, t, z_codes[:, cols], z_plane[:, cols])
+                nc.scalar.copy(result_windows[t][:, cols], a_banks[t][:, cols])
+                nc.sync.dma_start(a_plain[:, t, cols], result_windows[t][:, cols])
+
+        b_total_0 = keep.tile([P, S], F32, name="b_total_0", tag="y_gained3")
+        half_of_a(0)
+        add_looked_up_size(b_total_0[:], b_size, 0, n6_list)
+        half_of_a(1)
+
+        b_total_12 = keep.tile([P, 2, S], F32, name="b_total_12", tag="z_half1")
+        b_total_3 = keep.tile([P, S], F32, name="b_total_3", tag="z_woven", align_bytes=64)
+        b_total = [b_total_0[:], b_total_12[:, 0, :], b_total_12[:, 1, :], b_total_3[:]]
+        for t in range(1, SLABS):
+            add_looked_up_size(b_total[t], b_size, t, n6_list)
+        b_recip = slabs("b_recip")
+        b_root = keep.tile([P, SLABS, S], F32, name="b_root", tag="z_codes", align_bytes=64)
         for cols in halves:
-            for t in range(PACK):
-                reciprocal(b_recip[:, t, cols], (b_root if t else root)[:, t, cols], b_sum[t][:, cols])
+            for t in range(SLABS):
+                reciprocal(b_recip[:, t, cols], b_root[:, t, cols], b_total[t][:, cols])
+
         out_codes = keep.tile([P, S], U32, name="out_codes", align_bytes=64)
         out_plane = keep.tile([P, S], U8, name="out_plane", align_bytes=64)
-        out_rows = out_0.rearrange("(p t) c -> p t c", t=PACK)
+        out_slabs = out_0.rearrange("(p t) c -> p t c", t=SLABS)
         out_words = out_1[0].rearrange("p n t -> p (n t)").bitcast(I32)
-        rounded = []
-        for h in range(2):
+        out_woven = []
+        for h, copy in enumerate((nc.scalar.copy, nc.vector.tensor_copy)):
             cols = halves[h]
-            diff = keep.tile([P, PACK, HALF], F32, name="diff", tag="diff")
-            result = rows4("result%d" % h, HALF)
-            for t in range(PACK):
+            diff = slabs("diff", HALF)
+            out_half = slabs("out_half%d" % h, HALF)
+            for t in range(SLABS):
                 nc.vector.tensor_tensor(
-                    diff[:, t, :], vals[t][:].indirect(n5_t[:, half_lists[h]]), a_plain[:, t, cols], ALU.subtract
+                    diff[:, t, :],
+                    result_windows[t][:].indirect(n5_list[:, list_halves[h]]),
+                    a_plain[:, t, cols],
+                    ALU.subtract,
                 )
-            nc.vector.scalar_tensor_tensor(result[:], diff[:], -1.0, b_recip[:, :, cols], ALU.mult, ALU.mult)
-            nc.sync.dma_start(out_rows[:, :, cols], result[:])
-            half = keep.tile([P, PACK * HALF], BF16, name="out_bf16_%d" % h, align_bytes=64)
-            if h == 0:
-                nc.scalar.copy(woven_out(half), woven_in(result))
-            else:
-                nc.vector.tensor_copy(woven_out(half), woven_in(result))
-            rounded.append(half)
+            nc.vector.scalar_tensor_tensor(out_half[:], diff[:], -1.0, b_recip[:, :, cols], ALU.mult, ALU.mult)
+            nc.sync.dma_start(out_slabs[:, :, cols], out_half[:])
+            woven = keep.tile([P, SLABS * HALF], BF16, name="out_woven%d" % h, align_bytes=64)
+            weave(copy, woven[:], out_half[:])
+            out_woven.append(woven)
         for h in range(2):
             cols = halves[h]
-            nc.vector.quantize_mx(out=out_codes[:, cols].bitcast(FP8X4), scales=out_plane[:, cols], in_=rounded[h][:])
+            nc.vector.quantize_mx(out=out_codes[:, cols].bitcast(FP8X4), scales=out_plane[:, cols], in_=out_woven[h][:])
             nc.sync.dma_start(out_words[:, cols], out_codes[:, cols].bitcast(I32))
-        plane_rows = out_2[0].bitcast(I32)
-        for q in range(4):
+        out_scale_rows = out_2[0].bitcast(I32)
+        for q in range(QUADRANTS):
             engine = nc.scalar if q % 2 else nc.sync
-            engine.dma_start(plane_rows[4 * q : 4 * q + 4, :], out_plane[32 * q : 32 * q + 4, :].bitcast(I32))
+            engine.dma_start(out_scale_rows[4 * q : 4 * q + 4, :], out_plane[32 * q : 32 * q + 4, :].bitcast(I32))

from contextlib import ExitStack

import concourse.mybir as mybir

F32 = mybir.dt.float32
BF16 = mybir.dt.bfloat16
I32 = mybir.dt.int32
U32 = mybir.dt.uint32
U16 = mybir.dt.uint16
U8 = mybir.dt.uint8
FP8X4 = mybir.dt.float8_e4m3fn_x4
FP4X4 = mybir.dt.float4_e2m1fn_x4
ACT = mybir.ActivationFunctionType
ALU = mybir.AluOpType

P = 128
SLABS = 4
QUADRANTS = 4
T = 2048
S = 512
HALF = S // 2
LINE = 4
FLOPS = 3 * 2 * 512 * 512 * 512


def tile_picked_forknormbnorm2gmax_none_po_kernel(
    tc, x_words, x_scales, w1_words, w1_scales, gn, w2_words, w2_scales, gm, w3_words, w3_scales,
    offs, n1, n2, n3, n4, n5, n6, out_0, out_1, out_2,
):
    nc = tc.nc
    halves = [slice(HALF * h, HALF * (h + 1)) for h in range(2)]
    list_halves = [slice(HALF // 16 * h, HALF // 16 * (h + 1)) for h in range(2)]

    with ExitStack() as ctx:
        keep = ctx.enter_context(tc.tile_pool(name="keep", bufs=1))
        psum = ctx.enter_context(tc.psum_pool(name="psum", bufs=1))

        def load_list(name, src):
            tile = keep.tile([P, S // 16], U16, name=name)
            nc.sync.dma_start(tile[:], src)
            return tile

        def zeroed_plane(name, engine):
            tile = keep.tile([P, S], U8, name=name, align_bytes=64)
            engine.memset(tile[:].bitcast(I32), 0)
            return tile

        def load_plane(tile, src, quadrants, engine):
            rows = src[0].bitcast(I32)
            for q in quadrants:
                engine.dma_start(tile[32 * q : 32 * q + 4, :].bitcast(I32), rows[4 * q : 4 * q + 4, :])

        def load_words(name, src):
            tile = keep.tile([P, 2 * S], U8, name=name, align_bytes=64)
            nc.sync.dma_start(tile[:].bitcast(I32), src[0].bitcast(I32))
            return tile

        def load_gain(name, src):
            tile = keep.tile([P, SLABS], F32, name=name)
            nc.sync.dma_start(tile[:], src.rearrange("(p t) o -> p (t o)", t=SLABS))
            return tile

        def deal(name, words, plane):
            dealt_words = keep.tile([P, 2 * S], U8, name=name + "_words", align_bytes=64)
            dealt_plane = keep.tile([P, S], U8, name=name + "_plane", align_bytes=64)
            nc.gpsimd.tensor_copy(
                dealt_words[:].rearrange("p (t m b) -> p t m b", t=SLABS, b=2),
                words[:].rearrange("p (m t b) -> p t m b", t=SLABS, b=2),
            )
            nc.gpsimd.tensor_copy(
                dealt_plane[:].rearrange("p (t m) -> p t m", t=SLABS),
                plane[:].rearrange("p (m t) -> p t m", t=SLABS),
            )
            return dealt_words, dealt_plane

        def bank(number, width=S):
            return psum.tile([P, width], F32, name="bank", tag="bank%d" % number)

        def slab_product(out, weight, t, codes, plane):
            words, scales = weight
            nc.tensor.matmul_mx(
                out=out,
                lhsT=words[:, 2 * P * t : 2 * P * (t + 1)].bitcast(FP4X4),
                lhsT_scale=scales[:, P * t : P * (t + 1)],
                rhs=codes.bitcast(FP8X4),
                rhs_scale=plane,
                start=True,
                stop=True,
            )

        def slabs(name, width=S, tag=None):
            return keep.tile([P, SLABS, width], F32, name=name, tag=tag or name)

        def windows(name):
            return [
                keep.tile([P, 2 * S], F32, name=name, tag="%s%d" % (name, t), align_bytes=64) for t in range(SLABS)
            ]

        def weave(copy, woven, values):
            copy(
                woven.rearrange("p (c i t) -> p c t i", i=LINE, t=SLABS),
                values.rearrange("p t (c i) -> p c t i", i=LINE),
            )

        def sizes(size, values, which):
            for t in which:
                nc.scalar.activation(size[t][:, :S], values[t][:, :S], ACT.Abs)
                nc.sync.dma_start(size[t ^ 1][:, S:], size[t][:, :S])

        def add_looked_up_size(out, size, t, places):
            nc.vector.tensor_tensor(out, size[t][:].indirect(places[:]), size[t ^ 1][:, S:], ALU.add)

        def reciprocal(out, root, total):
            nc.scalar.activation(root, total, ACT.Abs_reciprocal_sqrt, bias=0.5)
            nc.scalar.activation(out, root, ACT.Square)

        x_plane_all = keep.tile([P, T], U8, name="x_plane_all", tag="x_plane_all", align_bytes=64)
        nc.vector.memset(x_plane_all[:, : T // 2].bitcast(I32), 0)
        nc.gpsimd.memset(x_plane_all[:, T // 2 :].bitcast(I32), 0)
        w1_plane = zeroed_plane("w1_plane_loaded", nc.vector)
        offs_list = load_list("offs", offs)
        w1_codes = load_words("w1_codes_loaded", w1_words)
        n4_list = load_list("n4", n4)
        load_plane(x_plane_all, x_scales, range(QUADRANTS // 2), nc.sync)
        load_plane(x_plane_all, x_scales, range(QUADRANTS // 2, QUADRANTS), nc.scalar)
        x_codes_all = keep.tile([P, T], U32, name="x_codes_all")
        nc.sync.dma_start(x_codes_all[:].bitcast(I32), x_words[0].rearrange("p n t -> p (n t)").bitcast(I32))
        load_plane(w1_plane, w1_scales, range(QUADRANTS), nc.sync)
        w3_plane = zeroed_plane("w3_plane_loaded", nc.gpsimd)
        w2_plane = zeroed_plane("w2_plane_loaded", nc.gpsimd)
        w3_codes = load_words("w3_codes_loaded", w3_words)
        n3_list = load_list("n3", n3)
        load_plane(w3_plane, w3_scales, range(QUADRANTS), nc.sync)
        gn_slabs = load_gain("gn", gn)
        w2_codes = load_words("w2_codes_loaded", w2_words)
        load_plane(w2_plane, w2_scales, range(QUADRANTS), nc.sync)
        gm_slabs = load_gain("gm", gm)
        n2_list = load_list("n2", n2)
        n1_list = load_list("n1", n1)
        n6_list = load_list("n6", n6)
        n5_list = load_list("n5", n5)

        result_windows = windows("result_window")
        nc.vector.memset(result_windows[0][:, S:], 0.0)
        for t in range(1, SLABS):
            nc.scalar.activation(result_windows[t][:, S:], result_windows[0][:, S:], ACT.Sigmoid)

        w1 = deal("w1", w1_codes, w1_plane)
        x_plane = keep.tile([P, S], U8, name="x_plane", align_bytes=64)
        nc.vector.tensor_copy(x_plane[:], x_plane_all[:].indirect(offs_list[:]))
        x_codes = keep.tile([P, S], U32, name="x_codes", tag="x_plane_all", align_bytes=64)
        for h in range(2):
            nc.vector.tensor_copy(x_codes[:, halves[h]], x_codes_all[:].indirect(offs_list[:, list_halves[h]]))
        pieces = [(t, cols) for cols in halves for t in (0, 1)] + [(t, slice(0, S)) for t in (2, 3)]
        last_piece_of_slab_0 = pieces.index((0, halves[1]))
        y_pieces = []
        for number, (t, cols) in enumerate(pieces):
            y_bank = bank(number, cols.stop - cols.start)
            slab_product(y_bank[:], w1, t, x_codes[:, cols], x_plane[:, cols])
            copy = nc.vector.tensor_copy if number <= last_piece_of_slab_0 else nc.scalar.copy
            copy(result_windows[t][:, cols], y_bank[:])
            y_pieces.append((t, cols, y_bank))
        w3 = deal("w3", w3_codes, w3_plane)

        y_n4 = slabs("y_n4")
        gate = slabs("gate")
        gated = slabs("gated")
        larger = slabs("larger")
        for t in range(SLABS):
            nc.vector.tensor_copy(y_n4[:, t, :], result_windows[t][:].indirect(n4_list[:]))
        y_size = windows("y_size")
        sizes(y_size, result_windows, (0, 1))
        for t in range(SLABS):
            nc.scalar.activation(gate[:, t, :], result_windows[t][:].indirect(n3_list[:]), ACT.Sigmoid)
        for t in range(SLABS + 1):
            for slab, cols, y_bank in y_pieces:
                if slab == t:
                    nc.vector.tensor_tensor(gated[:, t, cols], gate[:, t, cols], y_bank[:], ALU.mult)
            if t:
                nc.vector.tensor_tensor(larger[:, t - 1, :], gated[:, t - 1, :], y_n4[:, t - 1, :], ALU.max)
        sizes(y_size, result_windows, (2, 3))
        y_gained = [keep.tile([P, S], F32, name="y_gained", tag="y_gained%d" % t) for t in range(SLABS)]
        for t in range(SLABS):
            nc.gpsimd.tensor_scalar(
                y_gained[t][:], result_windows[t][:, :S], gn_slabs[:, t : t + 1], 0.0, ALU.mult, ALU.add
            )
        w2 = deal("w2", w2_codes, w2_plane)
        y_total = [keep.tile([P, S], F32, name="y_total%d" % t) for t in range(SLABS)]
        z2_slabs = keep.tile([P, SLABS, S], BF16, name="z2_slabs")
        for t in range(SLABS):
            nc.scalar.activation(z2_slabs[:, t, :], larger[:, t, :], ACT.Copy, scale=gm_slabs[:, t : t + 1])
        z2_codes = keep.tile([P, S], U32, name="z2_codes", align_bytes=64)
        z2_plane = keep.tile([P, S], U8, name="z2_plane", align_bytes=64)

        for t in (0, 1):
            add_looked_up_size(y_total[t][:], y_size, t, n2_list)
        z2_woven = keep.tile([P, SLABS * S], BF16, name="z2_woven", tag="y_size0", align_bytes=64)
        weave(nc.vector.tensor_copy, z2_woven[:], z2_slabs[:])
        nc.vector.quantize_mx(out=z2_codes[:].bitcast(FP8X4), scales=z2_plane[:], in_=z2_woven[:])
        for t in (2, 3):
            add_looked_up_size(y_total[t][:], y_size, t, n2_list)

        b_banks = [bank(SLABS + t) for t in range(SLABS)]
        for t in range(SLABS):
            slab_product(b_banks[t][:], w3, t, z2_codes[:], z2_plane[:])

        y_root = slabs("y_root", tag="z_half1")
        y_recip = slabs("y_recip")
        b_size = windows("b_size")
        for t in range(SLABS):
            reciprocal(y_recip[:, t, :], y_root[:, t, :], y_total[t][:])
        sizes(b_size, b_banks, range(SLABS))
        z_woven = keep.tile([P, SLABS * S], BF16, name="z_woven", tag="z_woven", align_bytes=64)
        woven_halves = [slice(SLABS * cols.start, SLABS * cols.stop) for cols in halves]
        for h in range(2):
            z_half = slabs("z_half", HALF, tag="z_half%d" % h)
            for t in range(SLABS):
                nc.vector.tensor_tensor(
                    z_half[:, t, :],
                    y_gained[t][:].indirect(n1_list[:, list_halves[h]]),
                    y_recip[:, t, halves[h]],
                    ALU.mult,
                )
            weave(nc.scalar.copy, z_woven[:, woven_halves[h]], z_half[:])

        z_codes = keep.tile([P, S], U32, name="z_codes", tag="z_codes", align_bytes=64)
        z_plane = keep.tile([P, S], U8, name="z_plane", align_bytes=64)
        a_banks = [bank(t) for t in range(SLABS)]
        a_plain = slabs("a_plain")

        def half_of_a(h):
            cols = halves[h]
            nc.vector.quantize_mx(
                out=z_codes[:, cols].bitcast(FP8X4), scales=z_plane[:, cols], in_=z_woven[:, woven_halves[h]]
            )
            for t in range(SLABS):
                slab_product(a_banks[t][:, cols], w2, t, z_codes[:, cols], z_plane[:, cols])
                nc.scalar.copy(result_windows[t][:, cols], a_banks[t][:, cols])
                nc.sync.dma_start(a_plain[:, t, cols], result_windows[t][:, cols])

        b_total_0 = keep.tile([P, S], F32, name="b_total_0", tag="y_gained3")
        half_of_a(0)
        add_looked_up_size(b_total_0[:], b_size, 0, n6_list)
        half_of_a(1)

        b_total_12 = keep.tile([P, 2, S], F32, name="b_total_12", tag="z_half1")
        b_total_3 = keep.tile([P, S], F32, name="b_total_3", tag="z_woven", align_bytes=64)
        b_total = [b_total_0[:], b_total_12[:, 0, :], b_total_12[:, 1, :], b_total_3[:]]
        for t in range(1, SLABS):
            add_looked_up_size(b_total[t], b_size, t, n6_list)
        b_recip = slabs("b_recip")
        b_root = keep.tile([P, SLABS, S], F32, name="b_root", tag="z_codes", align_bytes=64)
        for cols in halves:
            for t in range(SLABS):
                reciprocal(b_recip[:, t, cols], b_root[:, t, cols], b_total[t][:, cols])

        out_codes = keep.tile([P, S], U32, name="out_codes", align_bytes=64)
        out_plane = keep.tile([P, S], U8, name="out_plane", align_bytes=64)
        out_slabs = out_0.rearrange("(p t) c -> p t c", t=SLABS)
        out_words = out_1[0].rearrange("p n t -> p (n t)").bitcast(I32)
        out_woven = []
        for h, copy in enumerate((nc.scalar.copy, nc.vector.tensor_copy)):
            cols = halves[h]
            diff = slabs("diff", HALF)
            out_half = slabs("out_half%d" % h, HALF)
            for t in range(SLABS):
                nc.vector.tensor_tensor(
                    diff[:, t, :],
                    result_windows[t][:].indirect(n5_list[:, list_halves[h]]),
                    a_plain[:, t, cols],
                    ALU.subtract,
                )
            nc.vector.scalar_tensor_tensor(out_half[:], diff[:], -1.0, b_recip[:, :, cols], ALU.mult, ALU.mult)
            nc.sync.dma_start(out_slabs[:, :, cols], out_half[:])
            woven = keep.tile([P, SLABS * HALF], BF16, name="out_woven%d" % h, align_bytes=64)
            weave(copy, woven[:], out_half[:])
            out_woven.append(woven)
        for h in range(2):
            cols = halves[h]
            nc.vector.quantize_mx(out=out_codes[:, cols].bitcast(FP8X4), scales=out_plane[:, cols], in_=out_woven[h][:])
            nc.sync.dma_start(out_words[:, cols], out_codes[:, cols].bitcast(I32))
        out_scale_rows = out_2[0].bitcast(I32)
        for q in range(QUADRANTS):
            engine = nc.scalar if q % 2 else nc.sync
            engine.dma_start(out_scale_rows[4 * q : 4 * q + 4, :], out_plane[32 * q : 32 * q + 4, :].bitcast(I32))
